import numpy as np
import ml_dtypes


def mxq(x, axis, fmt="e4m3"):
    dtype, down = {"e4m3": (ml_dtypes.float8_e4m3fn, 7), "e5m2": (ml_dtypes.float8_e5m2, 14)}[fmt]
    v = np.moveaxis(np.asarray(x, np.float32).astype(ml_dtypes.bfloat16).astype(np.float64), axis, -1)
    blocks = v.reshape(v.shape[:-1] + (-1, 32))
    amax = np.abs(blocks).max(-1, keepdims=True)
    byte = np.maximum(np.where(amax > 0, np.frexp(amax)[1] - 1 + 127, 0) - down, 1)
    scale = np.exp2(byte - 127.0)
    codes = (blocks / scale).astype(np.float32).astype(dtype).astype(np.float64)
    return np.moveaxis((codes * scale).reshape(v.shape), -1, axis)


WIDE = False


def mx_kscale(k):
    if not WIDE:
        return np.ones(k)
    levels = np.array([10, -10, 5, -5, 0])
    if k % 512:
        return np.exp2(np.random.permutation(np.resize(levels, k // 32))).repeat(32)
    a = np.empty((k // 512, 16))
    for p in range(k // 512):
        a[p, :8] = np.random.permutation(np.resize(levels, 8))
        for g in range(8):
            far = levels[np.abs(levels - a[p, g]) >= 10]
            a[p, g + 8] = far[np.random.randint(len(far))]
    return np.exp2(a.ravel()).repeat(32)


def f64(x):
    return np.asarray(x).astype(np.float64)


def striped(idx):
    return np.tile(idx.reshape(-1, 16).T, (8, 1)).astype(np.uint16)


def unstriped(offs):
    return offs[:16].T.reshape(-1).astype(np.int64)


def pack_weight(w):
    k, n = w.shape
    w = f64(np.asarray(w, np.float32).astype(ml_dtypes.bfloat16)).reshape(k // 32, 32, n)
    amax = np.abs(w).max(1)
    byte = np.clip(np.where(amax > 0, np.frexp(amax)[1] - 1 + 127 - 7, 1), 1, 254)
    scaled = (w * np.exp2(127.0 - byte)[:, None, :]).reshape(k, n).astype(np.float32)
    words = np.ascontiguousarray(scaled.reshape(k // 512, 128, 4, n).transpose(0, 1, 3, 2)).astype(ml_dtypes.float8_e4m3fn).view(np.uint8)
    return words, np.ascontiguousarray(byte.astype(np.uint8).reshape(k // 512, 16, n))


def unpack_weight(words, scales):
    g, p, n, _ = words.shape
    vals = np.ascontiguousarray(words).view(ml_dtypes.float8_e4m3fn).astype(np.float64) * np.repeat(np.exp2(scales.astype(np.float64) - 127.0), 8, axis=1)[..., None]
    return vals.transpose(0, 1, 3, 2).reshape(g * 512, n)


def sigmoid(v):
    return 1.0 / (1.0 + np.exp(-np.maximum(v, -700.0)))


K, T, S, N, H = 512, 2048, 512, 512, 512


def setup_inputs():
    n = np.random.standard_normal
    s = mx_kscale(K)[:, None]
    u = mx_kscale(S)
    packed_xT = pack_weight(n((K, T)) * s)
    return {
        "x_words": packed_xT[0],
        "x_scales": packed_xT[1],
        "wa": (n((K, H)) / np.sqrt(K) / s).astype(np.float32),
        "wb": (n((K, N)) / np.sqrt(K) / s).astype(np.float32),
        "gt": (np.random.uniform(0.5, 1.5, (S, 1)) * u[:, None]).astype(np.float32),
        "gi": (np.random.uniform(0.5, 1.5, (S, 1)) / u[:, None]).astype(np.float32),
        "offs": striped(np.random.permutation(T)[:S]),
        "val_l": striped(np.random.permutation(T)[:S]),
    }


def reference(x_words, x_scales, wa, wb, gt, gi, offs, val_l):
    xq = unpack_weight(x_words, x_scales)[:, unstriped(offs)]
    a = xq.T @ mxq(f64(wa), 0, "e4m3")
    z = f64(gt) * sigmoid(a)
    x_val_l = unpack_weight(x_words, x_scales)[:, unstriped(val_l)]
    b = x_val_l.T @ mxq(f64(wb), 0, "e4m3")
    z2 = f64(gi) * b
    return 0.0625 * ((mxq(z, 0, "e4m3").T @ mxq(z2, 0, "e4m3")))

@@ -1,0 +1,196 @@
+from contextlib import ExitStack
+
+import concourse.mybir as mybir
+from concourse.masks import make_identity
+
+K, T, S, N, H = 512, 2048, 512, 512, 512
+FLOPS = 2 * S * K * H + 2 * S * K * N + 2 * H * S * N
+
+F32 = mybir.dt.float32
+BF16 = mybir.dt.bfloat16
+I32 = mybir.dt.int32
+U32 = mybir.dt.uint32
+U16 = mybir.dt.uint16
+U8 = mybir.dt.uint8
+FP8X4 = mybir.dt.float8_e4m3fn_x4
+ACT = mybir.ActivationFunctionType
+MULT = mybir.AluOpType.mult
+
+P = 128
+PACK = 4
+CH = 128
+HALF = 256
+
+
+def tile_picked_toklearn_sigmoid_p_kernel(
+    tc, x_words, x_scales, wa, wb, gt, gi, offs, val_l, out
+):
+    nc = tc.nc
+    with ExitStack() as ctx:
+        keep = ctx.enter_context(tc.tile_pool(name="keep", bufs=1))
+        psum = ctx.enter_context(tc.psum_pool(name="psum", bufs=4))
+
+        def sb(shape, dtype, name):
+            return keep.tile(shape, dtype, name=name, align_bytes=64)
+
+        val_list = sb([P, S // 16], U16, "val_list")
+        map_list = sb([P, S // 16], U16, "map_list")
+        scale_table = sb([P, T], U8, "scale_table")
+        word_table = sb([P, T], U32, "word_table")
+
+        nc.vector.memset(scale_table[:].bitcast(I32), 0)
+        nc.sync.dma_start(val_list[:], val_l)
+        nc.sync.dma_start(map_list[:], offs)
+        for q in range(4):
+            nc.sync.dma_start(
+                scale_table[32 * q : 32 * q + 4, :].bitcast(I32), x_scales[0, 4 * q : 4 * q + 4, :].bitcast(I32)
+            )
+        nc.sync.dma_start(
+            word_table[:].bitcast(I32), x_words[0].rearrange("p c r -> p (c r)").bitcast(I32)
+        )
+        rows = sb([P, P], F32, "rows")
+        nc.gpsimd.memset(rows[:], 0.0)
+        for r, g in enumerate((gi, gt)):
+            nc.sync.dma_start(
+                rows[PACK * r : PACK * (r + 1), :].rearrange("t (b q) -> t b q", q=8),
+                g.rearrange("(b t q) o -> t b (q o)", t=PACK, q=8),
+            )
+        raw = {}
+        for name, w in (("wb", wb), ("wa", wa)):
+            for h in range(2):
+                raw[name, h] = sb([P, PACK, HALF], F32, "raw_%s%d" % (name, h))
+                nc.sync.dma_start(
+                    raw[name, h][:], w[:, h * HALF : (h + 1) * HALF].rearrange("(p j) c -> p j c", j=PACK)
+                )
+
+        warm = sb([P, 2], F32, "warm")
+        nc.gpsimd.memset(warm[:, 0:1], 0.0)
+        nc.scalar.activation(warm[:, 1:2], warm[:, 0:1], ACT.Sigmoid)
+
+        ident = sb([P, P], F32, "ident")
+        make_identity(nc, ident[:])
+        turned = psum.tile([P, P], F32, name="turned", tag="a")
+        nc.tensor.transpose(turned[:], rows[:], ident[:])
+        place_w = sb([P, 2 * PACK], F32, "place_w")
+        nc.scalar.copy(place_w[:], turned[:, 0 : 2 * PACK])
+
+        def gather_scales(lst, name):
+            picked = sb([P, S], U8, name + "_picked")
+            nc.vector.tensor_copy(picked[:], scale_table[:].indirect(lst[:]))
+            return picked
+
+        def deal_scales(picked, name):
+            dealt = sb([P, S], U8, name + "_scales")
+            nc.vector.tensor_copy(
+                dealt[:].bitcast(I32).rearrange("p (t b q) -> p t b q", t=PACK, q=2),
+                picked[:].bitcast(I32).rearrange("p (b t q) -> p t b q", t=PACK, q=2),
+            )
+            return dealt
+
+        def gather_words(lst, name):
+            words = sb([P, S], U32, name + "_words")
+            nc.vector.tensor_copy(
+                words[:].rearrange("p (t b q) -> p b t q", t=PACK, q=8), word_table[:].indirect(lst[:])
+            )
+            return words
+
+        def cast(name, h):
+            grouped = sb([P, HALF, PACK], BF16, "grouped_%s%d" % (name, h))
+            nc.scalar.copy(
+                grouped[:].rearrange("p (c i) t -> p c t i", i=4),
+                raw[name, h][:].rearrange("p t (c i) -> p c t i", i=4),
+            )
+            return grouped
+
+        def quantize(grouped, width, name):
+            codes = sb([P, width], U32, name + "_codes")
+            scales = sb([P, width], U8, name + "_sc")
+            nc.vector.quantize_mx(
+                out=codes[:].bitcast(FP8X4), scales=scales[:], in_=grouped.rearrange("p c t -> p (c t)")
+            )
+            return codes, scales
+
+        def first_product(words, scales, wq, c, tag):
+            codes, wscales = wq[c // 2]
+            cols = slice((c % 2) * CH, (c % 2 + 1) * CH)
+            bank = psum.tile([P, PACK, CH], F32, name="bank_%s%d" % (tag, c), tag=tag)
+            for t in range(PACK):
+                nc.tensor.matmul_mx(
+                    out=bank[:, t, :],
+                    lhsT=words[:, t * P : (t + 1) * P].bitcast(FP8X4),
+                    lhsT_scale=scales[:, t * P : (t + 1) * P],
+                    rhs=codes[:, cols].bitcast(FP8X4),
+                    rhs_scale=wscales[:, cols],
+                    start=True,
+                    stop=True,
+                )
+            return bank
+
+        def spread(r):
+            return place_w[:, PACK * r : PACK * (r + 1)].unsqueeze(1).to_broadcast([P, CH, PACK])
+
+        val_picked = gather_scales(val_list, "val")
+        map_picked = gather_scales(map_list, "map")
+        val_scales = deal_scales(val_picked, "val")
+        map_scales = deal_scales(map_picked, "map")
+        val_words = gather_words(val_list, "val")
+        map_words = gather_words(map_list, "map")
+
+        wb_g = [cast("wb", h) for h in range(2)]
+        wa_g = [cast("wa", h) for h in range(2)]
+
+        z2 = sb([P, N, PACK], BF16, "values")
+        wb_q = []
+        wa_q = []
+        for h in range(2):
+            wb_q.append(quantize(wb_g[h][:], HALF, "wb%d" % h))
+            for c in (2 * h, 2 * h + 1):
+                bank = first_product(val_words, val_scales, wb_q, c, "b")
+                nc.vector.tensor_tensor(
+                    z2[:, c * CH : (c + 1) * CH, :], bank[:].rearrange("p t n -> p n t"), spread(0), MULT
+                )
+        wa_q.append(quantize(wa_g[0][:], HALF, "wa0"))
+        z2_codes, z2_scales = quantize(z2[:], N, "values")
+        wa_q.append(quantize(wa_g[1][:], HALF, "wa1"))
+
+        maps = []
+        for c in range(4):
+            bank = first_product(map_words, map_scales, wa_q, c, "a")
+            sig = sb([P, CH, PACK], F32, "sig%d" % c)
+            nc.scalar.activation(sig[:], bank[:].rearrange("p t n -> p n t"), ACT.Sigmoid)
+            maps.append(sig)
+
+        z = {}
+
+        def weigh(c):
+            z[c] = sb([P, CH, PACK], BF16, "z%d" % c)
+            nc.vector.tensor_tensor(z[c][:], maps[c][:], spread(1), MULT)
+
+        def finish(c):
+            codes, scales = quantize(z[c][:], CH, "z%d" % c)
+            result = sb([P, N], F32, "result%d" % c)
+            parts = 2 if c == 3 else 1
+            width = N // parts
+            for i in range(parts):
+                cols = slice(i * width, (i + 1) * width)
+                acc = psum.tile([P, width], F32, name="acc%d_%d" % (c, i), tag="b")
+                nc.tensor.matmul_mx(
+                    out=acc[:],
+                    lhsT=codes[:].bitcast(FP8X4),
+                    lhsT_scale=scales[:],
+                    rhs=z2_codes[:, cols].bitcast(FP8X4),
+                    rhs_scale=z2_scales[:, cols],
+                    start=True,
+                    stop=True,
+                )
+                if i == 0:
+                    nc.scalar.activation(result[:, cols], acc[:], ACT.Copy, scale=0.0625)
+                else:
+                    nc.vector.tensor_scalar_mul(result[:, cols], acc[:], 0.0625)
+                nc.sync.dma_start(out[c * CH : (c + 1) * CH, cols], result[:, cols])
+
+        weigh(0)
+        for c in range(1, 4):
+            weigh(c)
+            finish(c - 1)
+        finish(3)

@@ -38,54 +38,53 @@ def tile_picked_toklearn_sigmoid_p_kernel(
         scale_table = sb([P, T], U8, "scale_table")
         word_table = sb([P, T], U32, "word_table")
 
-        nc.vector.memset(scale_table[:].bitcast(I32), 0)
+        nc.gpsimd.memset(scale_table[:].bitcast(I32), 0)
+        rows = sb([P, P], F32, "rows")
+        nc.gpsimd.memset(rows[:], 0.0)
+        raw = {}
+
+        def load_weight(name, w, h):
+            raw[name, h] = sb([P, PACK, HALF], F32, "raw_%s%d" % (name, h))
+            nc.sync.dma_start(
+                raw[name, h][:], w[:, h * HALF : (h + 1) * HALF].rearrange("(p j) c -> p j c", j=PACK)
+            )
+
+        def load_gates():
+            for r, g in enumerate((gi, gt)):
+                nc.sync.dma_start(
+                    rows[PACK * r : PACK * (r + 1), :].rearrange("t (b q) -> t b q", q=8),
+                    g.rearrange("(b t q) o -> t b (q o)", t=PACK, q=8),
+                )
+
+        def load_words():
+            nc.sync.dma_start(
+                word_table[:].bitcast(I32), x_words[0].rearrange("p c r -> p (c r)").bitcast(I32)
+            )
+
         nc.sync.dma_start(val_list[:], val_l)
         nc.sync.dma_start(map_list[:], offs)
+        load_weight("wb", wb, 0)
         for q in range(4):
             nc.sync.dma_start(
                 scale_table[32 * q : 32 * q + 4, :].bitcast(I32), x_scales[0, 4 * q : 4 * q + 4, :].bitcast(I32)
             )
-        nc.sync.dma_start(
-            word_table[:].bitcast(I32), x_words[0].rearrange("p c r -> p (c r)").bitcast(I32)
-        )
-        rows = sb([P, P], F32, "rows")
-        nc.gpsimd.memset(rows[:], 0.0)
-        for r, g in enumerate((gi, gt)):
-            nc.sync.dma_start(
-                rows[PACK * r : PACK * (r + 1), :].rearrange("t (b q) -> t b q", q=8),
-                g.rearrange("(b t q) o -> t b (q o)", t=PACK, q=8),
-            )
-        raw = {}
-        for name, w in (("wb", wb), ("wa", wa)):
-            for h in range(2):
-                raw[name, h] = sb([P, PACK, HALF], F32, "raw_%s%d" % (name, h))
-                nc.sync.dma_start(
-                    raw[name, h][:], w[:, h * HALF : (h + 1) * HALF].rearrange("(p j) c -> p j c", j=PACK)
-                )
+        load_words()
+        load_gates()
+        load_weight("wb", wb, 1)
+        load_weight("wa", wa, 0)
+        load_weight("wa", wa, 1)
 
-        warm = sb([P, 2], F32, "warm")
-        nc.gpsimd.memset(warm[:, 0:1], 0.0)
-        nc.scalar.activation(warm[:, 1:2], warm[:, 0:1], ACT.Sigmoid)
 
         ident = sb([P, P], F32, "ident")
         make_identity(nc, ident[:])
-        turned = psum.tile([P, P], F32, name="turned", tag="a")
-        nc.tensor.transpose(turned[:], rows[:], ident[:])
+        first_bank = psum.tile([P, PACK, CH], F32, name="first_bank", tag="b")
+        turned = first_bank[:, 0, :]
+        nc.tensor.transpose(turned, rows[:], ident[:])
         place_w = sb([P, 2 * PACK], F32, "place_w")
         nc.scalar.copy(place_w[:], turned[:, 0 : 2 * PACK])
 
-        def gather_scales(lst, name):
-            picked = sb([P, S], U8, name + "_picked")
-            nc.vector.tensor_copy(picked[:], scale_table[:].indirect(lst[:]))
-            return picked
-
-        def deal_scales(picked, name):
-            dealt = sb([P, S], U8, name + "_scales")
-            nc.vector.tensor_copy(
-                dealt[:].bitcast(I32).rearrange("p (t b q) -> p t b q", t=PACK, q=2),
-                picked[:].bitcast(I32).rearrange("p (b t q) -> p t b q", t=PACK, q=2),
-            )
-            return dealt
+        picked = sb([P, 2, S], U8, "picked")
+        dealt = sb([P, 2, S], U8, "dealt")
 
         def gather_words(lst, name):
             words = sb([P, S], U32, name + "_words")
@@ -113,7 +112,10 @@ def tile_picked_toklearn_sigmoid_p_kernel(
         def first_product(words, scales, wq, c, tag):
             codes, wscales = wq[c // 2]
             cols = slice((c % 2) * CH, (c % 2 + 1) * CH)
-            bank = psum.tile([P, PACK, CH], F32, name="bank_%s%d" % (tag, c), tag=tag)
+            if tag == "b" and c == 0:
+                bank = first_bank
+            else:
+                bank = psum.tile([P, PACK, CH], F32, name="bank_%s%d" % (tag, c), tag=tag)
             for t in range(PACK):
                 nc.tensor.matmul_mx(
                     out=bank[:, t, :],
@@ -129,29 +131,44 @@ def tile_picked_toklearn_sigmoid_p_kernel(
         def spread(r):
             return place_w[:, PACK * r : PACK * (r + 1)].unsqueeze(1).to_broadcast([P, CH, PACK])
 
-        val_picked = gather_scales(val_list, "val")
-        map_picked = gather_scales(map_list, "map")
-        val_scales = deal_scales(val_picked, "val")
-        map_scales = deal_scales(map_picked, "map")
-        val_words = gather_words(val_list, "val")
-        map_words = gather_words(map_list, "map")
-
+        nc.vector.tensor_copy(picked[:, 0, :], scale_table[:].indirect(val_list[:]))
+        nc.vector.tensor_copy(picked[:, 1, :], scale_table[:].indirect(map_list[:]))
+        nc.vector.tensor_copy(
+            dealt[:].bitcast(I32).rearrange("p l (t b q) -> p l t b q", t=PACK, q=2),
+            picked[:].bitcast(I32).rearrange("p l (b t q) -> p l t b q", t=PACK, q=2),
+        )
+        val_scales = dealt[:, 0, :]
+        map_scales = dealt[:, 1, :]
         wb_g = [cast("wb", h) for h in range(2)]
         wa_g = [cast("wa", h) for h in range(2)]
-
-        z2 = sb([P, N, PACK], BF16, "values")
-        wb_q = []
+        wb_q = [quantize(wb_g[0][:], HALF, "wb0")]
+        val_words = gather_words(val_list, "val")
+        map_words = gather_words(map_list, "map")
+        wb_q.append(quantize(wb_g[1][:], HALF, "wb1"))
         wa_q = []
-        for h in range(2):
-            wb_q.append(quantize(wb_g[h][:], HALF, "wb%d" % h))
-            for c in (2 * h, 2 * h + 1):
-                bank = first_product(val_words, val_scales, wb_q, c, "b")
+        z2_codes = sb([P, N], U32, "values_codes")
+        z2_scales = sb([P, N], U8, "values_sc")
+
+        def weigh_values(h, stage):
+            for i in range(2):
+                bank = first_product(val_words, val_scales, wb_q, 2 * h + i, "b")
                 nc.vector.tensor_tensor(
-                    z2[:, c * CH : (c + 1) * CH, :], bank[:].rearrange("p t n -> p n t"), spread(0), MULT
+                    stage[:, i * CH : (i + 1) * CH, :], bank[:].rearrange("p t n -> p n t"), spread(0), MULT
                 )
+
+        def quantize_values(h, stage):
+            cols = slice(h * HALF, (h + 1) * HALF)
+            nc.vector.quantize_mx(
+                out=z2_codes[:, cols].bitcast(FP8X4), scales=z2_scales[:, cols], in_=stage[:].rearrange("p c t -> p (c t)")
+            )
+
+        weigh_values(0, wb_g[1])
         wa_q.append(quantize(wa_g[0][:], HALF, "wa0"))
-        z2_codes, z2_scales = quantize(z2[:], N, "values")
+        quantize_values(0, wb_g[1])
+        weigh_values(1, wa_g[0])
         wa_q.append(quantize(wa_g[1][:], HALF, "wa1"))
+        quantize_values(1, wa_g[0])
+
 
         maps = []
         for c in range(4):
@@ -169,7 +186,7 @@ def tile_picked_toklearn_sigmoid_p_kernel(
         def finish(c):
             codes, scales = quantize(z[c][:], CH, "z%d" % c)
             result = sb([P, N], F32, "result%d" % c)
-            parts = 2 if c == 3 else 1
+            parts = 2 if c >= 2 else 1
             width = N // parts
             for i in range(parts):
                 cols = slice(i * width, (i + 1) * width)
@@ -187,7 +204,10 @@ def tile_picked_toklearn_sigmoid_p_kernel(
                     nc.scalar.activation(result[:, cols], acc[:], ACT.Copy, scale=0.0625)
                 else:
                     nc.vector.tensor_scalar_mul(result[:, cols], acc[:], 0.0625)
-                nc.sync.dma_start(out[c * CH : (c + 1) * CH, cols], result[:, cols])
+                if c == 3:
+                    nc.sync.dma_start(out[c * CH : (c + 1) * CH, cols], result[:, cols])
+            if c < 3:
+                nc.sync.dma_start(out[c * CH : (c + 1) * CH, :], result[:])
 
         weigh(0)
         for c in range(1, 4):

@@ -38,9 +38,12 @@ def tile_picked_toklearn_sigmoid_p_kernel(
         scale_table = sb([P, T], U8, "scale_table")
         word_table = sb([P, T], U32, "word_table")
 
-        nc.gpsimd.memset(scale_table[:].bitcast(I32), 0)
-        rows = sb([P, P], F32, "rows")
-        nc.gpsimd.memset(rows[:], 0.0)
+        nc.vector.memset(scale_table[:].bitcast(I32), 0)
+        rows = sb([2, S], F32, "rows")
+        ident = sb([P, P], F32, "ident")
+        dealt_rows = sb([P, PACK, P], F32, "dealt_rows")
+        nc.vector.memset(ident[:], 0.0)
+        nc.vector.memset(dealt_rows[:], 0.0)
         raw = {}
 
         def load_weight(name, w, h):
@@ -51,10 +54,7 @@ def tile_picked_toklearn_sigmoid_p_kernel(
 
         def load_gates():
             for r, g in enumerate((gi, gt)):
-                nc.sync.dma_start(
-                    rows[PACK * r : PACK * (r + 1), :].rearrange("t (b q) -> t b q", q=8),
-                    g.rearrange("(b t q) o -> t b (q o)", t=PACK, q=8),
-                )
+                nc.sync.dma_start(rows[r : r + 1, :], g.rearrange("s o -> o s"))
 
         def load_words():
             nc.sync.dma_start(
@@ -63,25 +63,30 @@ def tile_picked_toklearn_sigmoid_p_kernel(
 
         nc.sync.dma_start(val_list[:], val_l)
         nc.sync.dma_start(map_list[:], offs)
-        load_weight("wb", wb, 0)
         for q in range(4):
             nc.sync.dma_start(
                 scale_table[32 * q : 32 * q + 4, :].bitcast(I32), x_scales[0, 4 * q : 4 * q + 4, :].bitcast(I32)
             )
-        load_words()
+        load_weight("wb", wb, 0)
         load_gates()
+        load_words()
         load_weight("wb", wb, 1)
         load_weight("wa", wa, 0)
         load_weight("wa", wa, 1)
 
 
-        ident = sb([P, P], F32, "ident")
-        make_identity(nc, ident[:])
+        make_identity(nc, ident[:], nomemset=True)
+        warm = sb([P, 1], F32, "warm")
+        nc.scalar.activation(warm[:], dealt_rows[:, 0, 0:1], ACT.Sigmoid)
+        nc.scalar.copy(
+            dealt_rows[0:2].rearrange("r t (b q) -> r t b q", q=8),
+            rows[:].rearrange("r (b t q) -> r t b q", t=PACK, q=8),
+        )
         first_bank = psum.tile([P, PACK, CH], F32, name="first_bank", tag="b")
-        turned = first_bank[:, 0, :]
-        nc.tensor.transpose(turned, rows[:], ident[:])
-        place_w = sb([P, 2 * PACK], F32, "place_w")
-        nc.scalar.copy(place_w[:], turned[:, 0 : 2 * PACK])
+        for t in range(PACK):
+            nc.tensor.transpose(first_bank[:, t, :], dealt_rows[:, t, :], ident[:])
+        place_w = sb([P, 2, PACK], F32, "place_w")
+        nc.scalar.copy(place_w[:], first_bank[:, :, 0:2].rearrange("p t r -> p r t"))
 
         picked = sb([P, 2, S], U8, "picked")
         dealt = sb([P, 2, S], U8, "dealt")
@@ -129,7 +134,7 @@ def tile_picked_toklearn_sigmoid_p_kernel(
             return bank
 
         def spread(r):
-            return place_w[:, PACK * r : PACK * (r + 1)].unsqueeze(1).to_broadcast([P, CH, PACK])
+            return place_w[:, r, :].unsqueeze(1).to_broadcast([P, CH, PACK])
 
         nc.vector.tensor_copy(picked[:, 0, :], scale_table[:].indirect(val_list[:]))
         nc.vector.tensor_copy(picked[:, 1, :], scale_table[:].indirect(map_list[:]))
@@ -152,9 +157,16 @@ def tile_picked_toklearn_sigmoid_p_kernel(
         def weigh_values(h, stage):
             for i in range(2):
                 bank = first_product(val_words, val_scales, wb_q, 2 * h + i, "b")
-                nc.vector.tensor_tensor(
-                    stage[:, i * CH : (i + 1) * CH, :], bank[:].rearrange("p t n -> p n t"), spread(0), MULT
-                )
+                part = stage[:, i * CH : (i + 1) * CH, :]
+                if 2 * h + i in ():
+                    planes = sb([P, PACK, CH], BF16, "planes%d" % (2 * h + i))
+                    for t in range(PACK):
+                        nc.scalar.activation(planes[:, t, :], bank[:, t, :], ACT.Copy, scale=place_w[:, t : t + 1])
+                    nc.scalar.copy(
+                        part.rearrange("p (c i) t -> p c t i", i=4), planes[:].rearrange("p t (c i) -> p c t i", i=4)
+                    )
+                else:
+                    nc.vector.tensor_tensor(part, bank[:].rearrange("p t n -> p n t"), spread(0), MULT)
 
         def quantize_values(h, stage):
             cols = slice(h * HALF, (h + 1) * HALF)

@@ -28,10 +28,14 @@ def tile_picked_toklearn_sigmoid_p_kernel(
     nc = tc.nc
     with ExitStack() as ctx:
         keep = ctx.enter_context(tc.tile_pool(name="keep", bufs=1))
+        shared = ctx.enter_context(tc.tile_pool(name="shared", bufs=1))
         psum = ctx.enter_context(tc.psum_pool(name="psum", bufs=4))
 
-        def sb(shape, dtype, name):
-            return keep.tile(shape, dtype, name=name, align_bytes=64)
+        def sb(shape, dtype, name, tag=None):
+            return keep.tile(shape, dtype, name=name, tag=tag or name, align_bytes=64)
+
+        def reused(shape, dtype, name, offset):
+            return shared.tile(shape, dtype, name=name, offset=offset, align_bytes=64)
 
         val_list = sb([P, S // 16], U16, "val_list")
         map_list = sb([P, S // 16], U16, "map_list")
@@ -39,9 +43,11 @@ def tile_picked_toklearn_sigmoid_p_kernel(
         word_table = sb([P, T], U32, "word_table")
 
         nc.vector.memset(scale_table[:].bitcast(I32), 0)
-        rows = sb([2, S], F32, "rows")
+        rows = reused([2, S], F32, "rows", 8192)
         ident = sb([P, P], F32, "ident")
         dealt_rows = sb([P, PACK, P], F32, "dealt_rows")
+        zero = sb([P, 1], F32, "zero")
+        nc.gpsimd.memset(zero[:], 0.0)
         nc.vector.memset(ident[:], 0.0)
         nc.vector.memset(dealt_rows[:], 0.0)
         raw = {}
@@ -62,14 +68,14 @@ def tile_picked_toklearn_sigmoid_p_kernel(
             )
 
         nc.sync.dma_start(val_list[:], val_l)
-        nc.sync.dma_start(map_list[:], offs)
+        load_weight("wb", wb, 0)
         for q in range(4):
             nc.sync.dma_start(
                 scale_table[32 * q : 32 * q + 4, :].bitcast(I32), x_scales[0, 4 * q : 4 * q + 4, :].bitcast(I32)
             )
-        load_weight("wb", wb, 0)
-        load_gates()
+        nc.sync.dma_start(map_list[:], offs)
         load_words()
+        load_gates()
         load_weight("wb", wb, 1)
         load_weight("wa", wa, 0)
         load_weight("wa", wa, 1)
@@ -77,7 +83,7 @@ def tile_picked_toklearn_sigmoid_p_kernel(
 
         make_identity(nc, ident[:], nomemset=True)
         warm = sb([P, 1], F32, "warm")
-        nc.scalar.activation(warm[:], dealt_rows[:, 0, 0:1], ACT.Sigmoid)
+        nc.scalar.activation(warm[:], zero[:], ACT.Sigmoid)
         nc.scalar.copy(
             dealt_rows[0:2].rearrange("r t (b q) -> r t b q", q=8),
             rows[:].rearrange("r (b t q) -> r t b q", t=PACK, q=8),
@@ -89,10 +95,9 @@ def tile_picked_toklearn_sigmoid_p_kernel(
         nc.scalar.copy(place_w[:], first_bank[:, :, 0:2].rearrange("p t r -> p r t"))
 
         picked = sb([P, 2, S], U8, "picked")
-        dealt = sb([P, 2, S], U8, "dealt")
+        dealt = reused([P, 2, S], U8, "dealt", 8192 + 64)
 
-        def gather_words(lst, name):
-            words = sb([P, S], U32, name + "_words")
+        def gather_words(lst, words):
             nc.vector.tensor_copy(
                 words[:].rearrange("p (t b q) -> p b t q", t=PACK, q=8), word_table[:].indirect(lst[:])
             )
@@ -107,7 +112,10 @@ def tile_picked_toklearn_sigmoid_p_kernel(
             return grouped
 
         def quantize(grouped, width, name):
-            codes = sb([P, width], U32, name + "_codes")
+            if name == "wb0":
+                codes = reused([P, width], U32, "wb0_codes", 8192 - 960)
+            else:
+                codes = sb([P, width], U32, name + "_codes")
             scales = sb([P, width], U8, name + "_sc")
             nc.vector.quantize_mx(
                 out=codes[:].bitcast(FP8X4), scales=scales[:], in_=grouped.rearrange("p c t -> p (c t)")
@@ -138,48 +146,33 @@ def tile_picked_toklearn_sigmoid_p_kernel(
 
         nc.vector.tensor_copy(picked[:, 0, :], scale_table[:].indirect(val_list[:]))
         nc.vector.tensor_copy(picked[:, 1, :], scale_table[:].indirect(map_list[:]))
+        wb_g = [cast("wb", h) for h in range(2)]
+        wa_g = [cast("wa", h) for h in range(2)]
+        val_words = gather_words(val_list, sb([P, S], U32, "val_words"))
         nc.vector.tensor_copy(
             dealt[:].bitcast(I32).rearrange("p l (t b q) -> p l t b q", t=PACK, q=2),
             picked[:].bitcast(I32).rearrange("p l (b t q) -> p l t b q", t=PACK, q=2),
         )
         val_scales = dealt[:, 0, :]
         map_scales = dealt[:, 1, :]
-        wb_g = [cast("wb", h) for h in range(2)]
-        wa_g = [cast("wa", h) for h in range(2)]
         wb_q = [quantize(wb_g[0][:], HALF, "wb0")]
-        val_words = gather_words(val_list, "val")
-        map_words = gather_words(map_list, "map")
+        map_words = gather_words(map_list, reused([P, S], U32, "map_words", 8192 + 64 + 1024))
         wb_q.append(quantize(wb_g[1][:], HALF, "wb1"))
         wa_q = []
         z2_codes = sb([P, N], U32, "values_codes")
         z2_scales = sb([P, N], U8, "values_sc")
 
-        def weigh_values(h, stage):
-            for i in range(2):
-                bank = first_product(val_words, val_scales, wb_q, 2 * h + i, "b")
-                part = stage[:, i * CH : (i + 1) * CH, :]
-                if 2 * h + i in ():
-                    planes = sb([P, PACK, CH], BF16, "planes%d" % (2 * h + i))
-                    for t in range(PACK):
-                        nc.scalar.activation(planes[:, t, :], bank[:, t, :], ACT.Copy, scale=place_w[:, t : t + 1])
-                    nc.scalar.copy(
-                        part.rearrange("p (c i) t -> p c t i", i=4), planes[:].rearrange("p t (c i) -> p c t i", i=4)
-                    )
-                else:
-                    nc.vector.tensor_tensor(part, bank[:].rearrange("p t n -> p n t"), spread(0), MULT)
-
-        def quantize_values(h, stage):
-            cols = slice(h * HALF, (h + 1) * HALF)
-            nc.vector.quantize_mx(
-                out=z2_codes[:, cols].bitcast(FP8X4), scales=z2_scales[:, cols], in_=stage[:].rearrange("p c t -> p (c t)")
-            )
-
-        weigh_values(0, wb_g[1])
+        values = sb([P, N, PACK], BF16, "values", tag="raw_wa0")
         wa_q.append(quantize(wa_g[0][:], HALF, "wa0"))
-        quantize_values(0, wb_g[1])
-        weigh_values(1, wa_g[0])
+        for c in range(4):
+            bank = first_product(val_words, val_scales, wb_q, c, "b")
+            nc.vector.tensor_tensor(
+                values[:, c * CH : (c + 1) * CH, :], bank[:].rearrange("p t n -> p n t"), spread(0), MULT
+            )
         wa_q.append(quantize(wa_g[1][:], HALF, "wa1"))
-        quantize_values(1, wa_g[0])
+        nc.vector.quantize_mx(
+            out=z2_codes[:].bitcast(FP8X4), scales=z2_scales[:], in_=values[:].rearrange("p c t -> p (c t)")
+        )
 
 
         maps = []

@@ -162,17 +162,21 @@ def tile_picked_toklearn_sigmoid_p_kernel(
         z2_codes = sb([P, N], U32, "values_codes")
         z2_scales = sb([P, N], U8, "values_sc")
 
-        values = sb([P, N, PACK], BF16, "values", tag="raw_wa0")
-        wa_q.append(quantize(wa_g[0][:], HALF, "wa0"))
-        for c in range(4):
-            bank = first_product(val_words, val_scales, wb_q, c, "b")
-            nc.vector.tensor_tensor(
-                values[:, c * CH : (c + 1) * CH, :], bank[:].rearrange("p t n -> p n t"), spread(0), MULT
+        values = [sb([P, HALF, PACK], BF16, "values%d" % h, tag=("raw_wb1", "raw_wa0")[h]) for h in range(2)]
+        for h in range(2):
+            for i in range(2):
+                bank = first_product(val_words, val_scales, wb_q, 2 * h + i, "b")
+                nc.vector.tensor_tensor(
+                    values[h][:, i * CH : (i + 1) * CH, :], bank[:].rearrange("p t n -> p n t"), spread(0), MULT
+                )
+            wa_q.append(quantize(wa_g[h][:], HALF, "wa%d" % h))
+        for h in range(2):
+            cols = slice(h * HALF, (h + 1) * HALF)
+            nc.vector.quantize_mx(
+                out=z2_codes[:, cols].bitcast(FP8X4),
+                scales=z2_scales[:, cols],
+                in_=values[h][:].rearrange("p c t -> p (c t)"),
             )
-        wa_q.append(quantize(wa_g[1][:], HALF, "wa1"))
-        nc.vector.quantize_mx(
-            out=z2_codes[:].bitcast(FP8X4), scales=z2_scales[:], in_=values[:].rearrange("p c t -> p (c t)")
-        )
 
 
         maps = []

@@ -20,6 +20,11 @@ P = 128
 PACK = 4
 CH = 128
 HALF = 256
+BANKS = {
+    "b": ("b01", "b01", "b2", "b3"),
+    "a": ("a0", "b01", "b2", "b3"),
+    "out": (("r0", "a0"), ("r1",), ("b01", "r0"), ("b01", "b2")),
+}
 
 
 def tile_picked_toklearn_sigmoid_p_kernel(
@@ -29,7 +34,7 @@ def tile_picked_toklearn_sigmoid_p_kernel(
     with ExitStack() as ctx:
         keep = ctx.enter_context(tc.tile_pool(name="keep", bufs=1))
         shared = ctx.enter_context(tc.tile_pool(name="shared", bufs=1))
-        psum = ctx.enter_context(tc.psum_pool(name="psum", bufs=4))
+        psum = ctx.enter_context(tc.psum_pool(name="psum", bufs=1))
 
         def sb(shape, dtype, name, tag=None):
             return keep.tile(shape, dtype, name=name, tag=tag or name, align_bytes=64)
@@ -53,7 +58,10 @@ def tile_picked_toklearn_sigmoid_p_kernel(
         raw = {}
 
         def load_weight(name, w, h):
-            raw[name, h] = sb([P, PACK, HALF], F32, "raw_%s%d" % (name, h))
+            if (name, h) == ("wa", 1):
+                raw[name, h] = reused([P, PACK, HALF], F32, "raw_wa1", 2048)
+            else:
+                raw[name, h] = sb([P, PACK, HALF], F32, "raw_%s%d" % (name, h))
             nc.sync.dma_start(
                 raw[name, h][:], w[:, h * HALF : (h + 1) * HALF].rearrange("(p j) c -> p j c", j=PACK)
             )
@@ -76,8 +84,8 @@ def tile_picked_toklearn_sigmoid_p_kernel(
         nc.sync.dma_start(map_list[:], offs)
         load_words()
         load_gates()
-        load_weight("wb", wb, 1)
         load_weight("wa", wa, 0)
+        load_weight("wb", wb, 1)
         load_weight("wa", wa, 1)
 
 
@@ -88,9 +96,12 @@ def tile_picked_toklearn_sigmoid_p_kernel(
             dealt_rows[0:2].rearrange("r t (b q) -> r t b q", q=8),
             rows[:].rearrange("r (b t q) -> r t b q", t=PACK, q=8),
         )
-        first_bank = psum.tile([P, PACK, CH], F32, name="first_bank", tag="b")
+        first_bank = psum.tile([P, PACK, CH], F32, name="first_bank", tag="b01", bufs=2)
         for t in range(PACK):
             nc.tensor.transpose(first_bank[:, t, :], dealt_rows[:, t, :], ident[:])
+        gate_bank = psum.tile([P, PACK, CH], F32, name="gate_bank")
+        for t in range(PACK):
+            nc.tensor.transpose(gate_bank[:, t, :], dealt_rows[:, t, :], ident[:])
         place_w = sb([P, 2, PACK], F32, "place_w")
         nc.scalar.copy(place_w[:], first_bank[:, :, 0:2].rearrange("p t r -> p r t"))
 
@@ -128,7 +139,7 @@ def tile_picked_toklearn_sigmoid_p_kernel(
             if tag == "b" and c == 0:
                 bank = first_bank
             else:
-                bank = psum.tile([P, PACK, CH], F32, name="bank_%s%d" % (tag, c), tag=tag)
+                bank = psum.tile([P, PACK, CH], F32, name="bank_%s%d" % (tag, c), tag=BANKS[tag][c], bufs=2 if BANKS[tag][c] == "b01" else 1)
             for t in range(PACK):
                 nc.tensor.matmul_mx(
                     out=bank[:, t, :],
@@ -146,8 +157,10 @@ def tile_picked_toklearn_sigmoid_p_kernel(
 
         nc.vector.tensor_copy(picked[:, 0, :], scale_table[:].indirect(val_list[:]))
         nc.vector.tensor_copy(picked[:, 1, :], scale_table[:].indirect(map_list[:]))
-        wb_g = [cast("wb", h) for h in range(2)]
-        wa_g = [cast("wa", h) for h in range(2)]
+        wb_g = [cast("wb", 0)]
+        wa_g = [cast("wa", 0)]
+        wb_g.append(cast("wb", 1))
+        wa_g.append(cast("wa", 1))
         val_words = gather_words(val_list, sb([P, S], U32, "val_words"))
         nc.vector.tensor_copy(
             dealt[:].bitcast(I32).rearrange("p l (t b q) -> p l t b q", t=PACK, q=2),
@@ -157,20 +170,20 @@ def tile_picked_toklearn_sigmoid_p_kernel(
         map_scales = dealt[:, 1, :]
         wb_q = [quantize(wb_g[0][:], HALF, "wb0")]
         map_words = gather_words(map_list, reused([P, S], U32, "map_words", 8192 + 64 + 1024))
-        wb_q.append(quantize(wb_g[1][:], HALF, "wb1"))
-        wa_q = []
+        wa_q = [quantize(wa_g[0][:], HALF, "wa0")]
         z2_codes = sb([P, N], U32, "values_codes")
         z2_scales = sb([P, N], U8, "values_sc")
 
-        values = [sb([P, HALF, PACK], BF16, "values%d" % h, tag=("raw_wb1", "raw_wa0")[h]) for h in range(2)]
-        for h in range(2):
+        values = [sb([P, HALF, PACK], BF16, "values0"), reused([P, HALF, PACK], BF16, "values1", 3072)]
+
+        def weigh_values(h):
             for i in range(2):
                 bank = first_product(val_words, val_scales, wb_q, 2 * h + i, "b")
                 nc.vector.tensor_tensor(
                     values[h][:, i * CH : (i + 1) * CH, :], bank[:].rearrange("p t n -> p n t"), spread(0), MULT
                 )
-            wa_q.append(quantize(wa_g[h][:], HALF, "wa%d" % h))
-        for h in range(2):
+
+        def quantize_values(h):
             cols = slice(h * HALF, (h + 1) * HALF)
             nc.vector.quantize_mx(
                 out=z2_codes[:, cols].bitcast(FP8X4),
@@ -178,28 +191,51 @@ def tile_picked_toklearn_sigmoid_p_kernel(
                 in_=values[h][:].rearrange("p c t -> p (c t)"),
             )
 
+        weigh_values(0)
+        wb_q.append(quantize(wb_g[1][:], HALF, "wb1"))
+        quantize_values(0)
+        wa_q.append(quantize(wa_g[1][:], HALF, "wa1"))
+        weigh_values(1)
+
 
         maps = []
         for c in range(4):
             bank = first_product(map_words, map_scales, wa_q, c, "a")
-            sig = sb([P, CH, PACK], F32, "sig%d" % c)
+            if c < 2:
+                sig = reused([P, CH, PACK], F32, "sig%d" % c, (1024, 5120)[c])
+            else:
+                sig = sb([P, CH, PACK], F32, "sig%d" % c)
             nc.scalar.activation(sig[:], bank[:].rearrange("p t n -> p n t"), ACT.Sigmoid)
             maps.append(sig)
 
         z = {}
 
         def weigh(c):
+            if c == 0:
+                z[c] = sb([P, CH, PACK], BF16, "z0", tag="grouped_wa1")
+                nc.gpsimd.tensor_tensor(z[c][:], maps[c][:], spread(1), MULT)
+                return
             z[c] = sb([P, CH, PACK], BF16, "z%d" % c)
-            nc.vector.tensor_tensor(z[c][:], maps[c][:], spread(1), MULT)
+            gate = spread(1)
+            if c == 1:
+                gate = gate_bank[:, :, 1:2].rearrange("p t o -> p o t").to_broadcast([P, CH, PACK])
+            nc.vector.tensor_tensor(z[c][:], maps[c][:], gate, MULT)
 
-        def finish(c):
-            codes, scales = quantize(z[c][:], CH, "z%d" % c)
-            result = sb([P, N], F32, "result%d" % c)
-            parts = 2 if c >= 2 else 1
+        zq = {}
+        results = {}
+
+        def quantize_map(c):
+            zq[c] = quantize(z[c][:], CH, "z%d" % c)
+            results[c] = sb([P, N], F32, "result%d" % c)
+
+        def finish(c, which=None):
+            codes, scales = zq[c]
+            result = results[c]
+            parts = 1 if c == 1 else 2
             width = N // parts
-            for i in range(parts):
+            for i in range(parts) if which is None else (which,):
                 cols = slice(i * width, (i + 1) * width)
-                acc = psum.tile([P, width], F32, name="acc%d_%d" % (c, i), tag="b")
+                acc = psum.tile([P, width], F32, name="acc%d_%d" % (c, i), tag=BANKS["out"][c][i], bufs=2 if BANKS["out"][c][i] == "b01" else 1)
                 nc.tensor.matmul_mx(
                     out=acc[:],
                     lhsT=codes[:].bitcast(FP8X4),
@@ -209,17 +245,25 @@ def tile_picked_toklearn_sigmoid_p_kernel(
                     start=True,
                     stop=True,
                 )
-                if i == 0:
+                if i == 0 or c == 0:
                     nc.scalar.activation(result[:, cols], acc[:], ACT.Copy, scale=0.0625)
                 else:
                     nc.vector.tensor_scalar_mul(result[:, cols], acc[:], 0.0625)
-                if c == 3:
+                if c != 1:
                     nc.sync.dma_start(out[c * CH : (c + 1) * CH, cols], result[:, cols])
-            if c < 3:
+            if c == 1:
                 nc.sync.dma_start(out[c * CH : (c + 1) * CH, :], result[:])
 
         weigh(0)
-        for c in range(1, 4):
-            weigh(c)
-            finish(c - 1)
+        weigh(1)
+        quantize_values(1)
+        quantize_map(0)
+        quantize_map(1)
+        finish(0)
+        finish(1)
+        weigh(2)
+        weigh(3)
+        quantize_map(2)
+        quantize_map(3)
+        finish(2)
         finish(3)

@@ -22,8 +22,8 @@ CH = 128
 HALF = 256
 BANKS = {
     "b": ("b01", "b01", "b2", "b3"),
-    "a": ("a0", "b01", "b2", "b3"),
-    "out": (("r0", "a0"), ("r1",), ("b01", "r0"), ("b01", "b2")),
+    "a": ("a0", "b01", "b01", "b2"),
+    "out": (("r0", "a0"), ("r1",), ("b01", "b3"), ("b01", "b2")),
 }
 
 
@@ -77,10 +77,8 @@ def tile_picked_toklearn_sigmoid_p_kernel(
 
         nc.sync.dma_start(val_list[:], val_l)
         load_weight("wb", wb, 0)
-        for q in range(4):
-            nc.sync.dma_start(
-                scale_table[32 * q : 32 * q + 4, :].bitcast(I32), x_scales[0, 4 * q : 4 * q + 4, :].bitcast(I32)
-            )
+        for r in range(4):
+            nc.sync.dma_start(scale_table[r:P:32, :].bitcast(I32), x_scales[0, r:16:4, :].bitcast(I32))
         nc.sync.dma_start(map_list[:], offs)
         load_words()
         load_gates()
@@ -215,11 +213,15 @@ def tile_picked_toklearn_sigmoid_p_kernel(
                 z[c] = sb([P, CH, PACK], BF16, "z0", tag="grouped_wa1")
                 nc.gpsimd.tensor_tensor(z[c][:], maps[c][:], spread(1), MULT)
                 return
-            z[c] = sb([P, CH, PACK], BF16, "z%d" % c)
-            gate = spread(1)
-            if c == 1:
-                gate = gate_bank[:, :, 1:2].rearrange("p t o -> p o t").to_broadcast([P, CH, PACK])
-            nc.vector.tensor_tensor(z[c][:], maps[c][:], gate, MULT)
+            z[c] = sb([P, CH, PACK], BF16, "z%d" % c, tag="grouped_wa1" if c == 3 else None)
+            width = CH
+            if c == 3:
+                width = CH // 2
+                nc.gpsimd.tensor_tensor(
+                    z[c][:, width:, :], maps[c][:, width:, :], spread(1)[:, width:, :], MULT
+                )
+            gate = gate_bank[:, :, 1:2].rearrange("p t o -> p o t").to_broadcast([P, width, PACK])
+            nc.vector.tensor_tensor(z[c][:, :width, :], maps[c][:, :width, :], gate, MULT)
 
         zq = {}
         results = {}

@@ -206,6 +206,18 @@ def tile_picked_toklearn_sigmoid_p_kernel(
             nc.scalar.activation(sig[:], bank[:].rearrange("p t n -> p n t"), ACT.Sigmoid)
             maps.append(sig)
 
+        idle_bank = psum.tile([P, S], F32, name="idle_bank", tag="b3")
+        for i in range(2):
+            nc.tensor.matmul_mx(
+                out=idle_bank[:],
+                lhsT=wa_q[1][0][:, i * CH : (i + 1) * CH].bitcast(FP8X4),
+                lhsT_scale=wa_q[1][1][:, i * CH : (i + 1) * CH],
+                rhs=map_words[:].bitcast(FP8X4),
+                rhs_scale=map_scales,
+                start=True,
+                stop=True,
+            )
+
         z = {}
 
         def weigh(c):

@@ -75,11 +75,11 @@ def tile_picked_toklearn_sigmoid_p_kernel(
                 word_table[:].bitcast(I32), x_words[0].rearrange("p c r -> p (c r)").bitcast(I32)
             )
 
-        nc.sync.dma_start(val_list[:], val_l)
         load_weight("wb", wb, 0)
+        nc.sync.dma_start(val_list[:], val_l)
+        nc.sync.dma_start(map_list[:], offs)
         for r in range(4):
             nc.sync.dma_start(scale_table[r:P:32, :].bitcast(I32), x_scales[0, r:16:4, :].bitcast(I32))
-        nc.sync.dma_start(map_list[:], offs)
         load_words()
         load_gates()
         load_weight("wa", wa, 0)
@@ -225,7 +225,10 @@ def tile_picked_toklearn_sigmoid_p_kernel(
                 z[c] = sb([P, CH, PACK], BF16, "z0", tag="grouped_wa1")
                 nc.gpsimd.tensor_tensor(z[c][:], maps[c][:], spread(1), MULT)
                 return
-            z[c] = sb([P, CH, PACK], BF16, "z%d" % c, tag="grouped_wa1" if c == 3 else None)
+            if c == 3:
+                z[c] = reused([P, CH, PACK], BF16, "z3", 3072)
+            else:
+                z[c] = sb([P, CH, PACK], BF16, "z%d" % c)
             width = CH
             if c == 3:
                 width = CH // 2
@@ -270,10 +273,11 @@ def tile_picked_toklearn_sigmoid_p_kernel(
 
         weigh(0)
         weigh(1)
-        quantize_values(1)
         quantize_map(0)
+        finish(0, 0)
+        quantize_values(1)
+        finish(0, 1)
         quantize_map(1)
-        finish(0)
         finish(1)
         weigh(2)
         weigh(3)

@@ -51,8 +51,6 @@ def tile_picked_toklearn_sigmoid_p_kernel(
         rows = reused([2, S], F32, "rows", 8192)
         ident = sb([P, P], F32, "ident")
         dealt_rows = sb([P, PACK, P], F32, "dealt_rows")
-        zero = sb([P, 1], F32, "zero")
-        nc.gpsimd.memset(zero[:], 0.0)
         nc.vector.memset(ident[:], 0.0)
         nc.vector.memset(dealt_rows[:], 0.0)
         raw = {}
@@ -89,7 +87,7 @@ def tile_picked_toklearn_sigmoid_p_kernel(
 
         make_identity(nc, ident[:], nomemset=True)
         warm = sb([P, 1], F32, "warm")
-        nc.scalar.activation(warm[:], zero[:], ACT.Sigmoid)
+        nc.scalar.activation(warm[:], dealt_rows[:, 0, 0:1], ACT.Sigmoid)
         nc.scalar.copy(
             dealt_rows[0:2].rearrange("r t (b q) -> r t b q", q=8),
             rows[:].rearrange("r (b t q) -> r t b q", t=PACK, q=8),
@@ -266,9 +264,9 @@ def tile_picked_toklearn_sigmoid_p_kernel(
                     nc.scalar.activation(result[:, cols], acc[:], ACT.Copy, scale=0.0625)
                 else:
                     nc.vector.tensor_scalar_mul(result[:, cols], acc[:], 0.0625)
-                if c != 1:
+                if c % 2 == 0:
                     nc.sync.dma_start(out[c * CH : (c + 1) * CH, cols], result[:, cols])
-            if c == 1:
+            if c % 2 == 1:
                 nc.sync.dma_start(out[c * CH : (c + 1) * CH, :], result[:])
 
         weigh(0)

@@ -92,23 +92,15 @@ def tile_picked_toklearn_sigmoid_p_kernel(
             dealt_rows[0:2].rearrange("r t (b q) -> r t b q", q=8),
             rows[:].rearrange("r (b t q) -> r t b q", t=PACK, q=8),
         )
-        first_bank = psum.tile([P, PACK, CH], F32, name="first_bank", tag="b01", bufs=2)
-        for t in range(PACK):
-            nc.tensor.transpose(first_bank[:, t, :], dealt_rows[:, t, :], ident[:])
         gate_bank = psum.tile([P, PACK, CH], F32, name="gate_bank")
         for t in range(PACK):
             nc.tensor.transpose(gate_bank[:, t, :], dealt_rows[:, t, :], ident[:])
-        place_w = sb([P, 2, PACK], F32, "place_w")
-        nc.scalar.copy(place_w[:], first_bank[:, :, 0:2].rearrange("p t r -> p r t"))
 
-        picked = sb([P, 2, S], U8, "picked")
-        dealt = reused([P, 2, S], U8, "dealt", 8192 + 64)
-
-        def gather_words(lst, words):
+        def gather(table, lst, dst):
             nc.vector.tensor_copy(
-                words[:].rearrange("p (t b q) -> p b t q", t=PACK, q=8), word_table[:].indirect(lst[:])
+                dst[:].rearrange("p (t b q) -> p b t q", t=PACK, q=8), table[:].indirect(lst[:])
             )
-            return words
+            return dst
 
         def cast(name, h):
             grouped = sb([P, HALF, PACK], BF16, "grouped_%s%d" % (name, h))
@@ -132,10 +124,7 @@ def tile_picked_toklearn_sigmoid_p_kernel(
         def first_product(words, scales, wq, c, tag):
             codes, wscales = wq[c // 2]
             cols = slice((c % 2) * CH, (c % 2 + 1) * CH)
-            if tag == "b" and c == 0:
-                bank = first_bank
-            else:
-                bank = psum.tile([P, PACK, CH], F32, name="bank_%s%d" % (tag, c), tag=BANKS[tag][c], bufs=2 if BANKS[tag][c] == "b01" else 1)
+            bank = psum.tile([P, PACK, CH], F32, name="bank_%s%d" % (tag, c), tag=BANKS[tag][c], bufs=2 if BANKS[tag][c] == "b01" else 1)
             for t in range(PACK):
                 nc.tensor.matmul_mx(
                     out=bank[:, t, :],
@@ -151,21 +140,17 @@ def tile_picked_toklearn_sigmoid_p_kernel(
         def spread(r):
             return place_w[:, r, :].unsqueeze(1).to_broadcast([P, CH, PACK])
 
-        nc.vector.tensor_copy(picked[:, 0, :], scale_table[:].indirect(val_list[:]))
-        nc.vector.tensor_copy(picked[:, 1, :], scale_table[:].indirect(map_list[:]))
+        val_scales = gather(scale_table, val_list, sb([P, S], U8, "val_scales"))
+        map_scales = gather(scale_table, map_list, sb([P, S], U8, "map_scales"))
         wb_g = [cast("wb", 0)]
         wa_g = [cast("wa", 0)]
+        place_w = sb([P, 2, PACK], F32, "place_w", tag="raw_wa0")
+        nc.scalar.copy(place_w[:], gate_bank[:, :, 0:2].rearrange("p t r -> p r t"))
         wb_g.append(cast("wb", 1))
         wa_g.append(cast("wa", 1))
-        val_words = gather_words(val_list, sb([P, S], U32, "val_words"))
-        nc.vector.tensor_copy(
-            dealt[:].bitcast(I32).rearrange("p l (t b q) -> p l t b q", t=PACK, q=2),
-            picked[:].bitcast(I32).rearrange("p l (b t q) -> p l t b q", t=PACK, q=2),
-        )
-        val_scales = dealt[:, 0, :]
-        map_scales = dealt[:, 1, :]
+        val_words = gather(word_table, val_list, sb([P, S], U32, "val_words"))
         wb_q = [quantize(wb_g[0][:], HALF, "wb0")]
-        map_words = gather_words(map_list, reused([P, S], U32, "map_words", 8192 + 64 + 1024))
+        map_words = gather(word_table, map_list, reused([P, S], U32, "map_words", 8192 + 64 + 1024))
         wa_q = [quantize(wa_g[0][:], HALF, "wa0")]
         z2_codes = sb([P, N], U32, "values_codes")
         z2_scales = sb([P, N], U8, "values_sc")
@@ -204,14 +189,14 @@ def tile_picked_toklearn_sigmoid_p_kernel(
             nc.scalar.activation(sig[:], bank[:].rearrange("p t n -> p n t"), ACT.Sigmoid)
             maps.append(sig)
 
-        idle_bank = psum.tile([P, S], F32, name="idle_bank", tag="b3")
+        idle_bank = psum.tile([P, 2, HALF], F32, name="idle_bank", tag="b3")
         for i in range(2):
             nc.tensor.matmul_mx(
-                out=idle_bank[:],
+                out=idle_bank[:, i, :],
                 lhsT=wa_q[1][0][:, i * CH : (i + 1) * CH].bitcast(FP8X4),
                 lhsT_scale=wa_q[1][1][:, i * CH : (i + 1) * CH],
-                rhs=map_words[:].bitcast(FP8X4),
-                rhs_scale=map_scales,
+                rhs=wb_q[i][0][:].bitcast(FP8X4),
+                rhs_scale=wb_q[i][1][:],
                 start=True,
                 stop=True,
             )

@@ -145,12 +145,12 @@ def tile_picked_toklearn_sigmoid_p_kernel(
         wb_g = [cast("wb", 0)]
         wa_g = [cast("wa", 0)]
         place_w = sb([P, 2, PACK], F32, "place_w", tag="raw_wa0")
-        nc.scalar.copy(place_w[:], gate_bank[:, :, 0:2].rearrange("p t r -> p r t"))
         wb_g.append(cast("wb", 1))
         wa_g.append(cast("wa", 1))
         val_words = gather(word_table, val_list, sb([P, S], U32, "val_words"))
         wb_q = [quantize(wb_g[0][:], HALF, "wb0")]
         map_words = gather(word_table, map_list, reused([P, S], U32, "map_words", 8192 + 64 + 1024))
+        nc.vector.tensor_copy(place_w[:], gate_bank[:, :, 0:2].rearrange("p t r -> p r t"))
         wa_q = [quantize(wa_g[0][:], HALF, "wa0")]
         z2_codes = sb([P, N], U32, "values_codes")
         z2_scales = sb([P, N], U8, "values_sc")

@@ -48,11 +48,13 @@ def tile_picked_toklearn_sigmoid_p_kernel(
         word_table = sb([P, T], U32, "word_table")
 
         nc.vector.memset(scale_table[:].bitcast(I32), 0)
-        rows = reused([2, S], F32, "rows", 8192)
         ident = sb([P, P], F32, "ident")
-        dealt_rows = sb([P, PACK, P], F32, "dealt_rows")
+        gate_row = reused([P, S], F32, "gate_row", 8192)
+        place_w = [sb([P, PACK], F32, "place_w%d" % r) for r in range(2)]
         nc.vector.memset(ident[:], 0.0)
-        nc.vector.memset(dealt_rows[:], 0.0)
+        nc.vector.memset(gate_row[:], 0.0)
+        warm = sb([P, 1], F32, "warm")
+        nc.scalar.activation(warm[:], gate_row[:, 0:1], ACT.Sigmoid)
         raw = {}
 
         def load_weight(name, w, h):
@@ -65,8 +67,8 @@ def tile_picked_toklearn_sigmoid_p_kernel(
             )
 
         def load_gates():
-            for r, g in enumerate((gi, gt)):
-                nc.sync.dma_start(rows[r : r + 1, :], g.rearrange("s o -> o s"))
+            nc.sync.dma_start(place_w[0][:], gi.rearrange("(p t) o -> p (t o)", t=PACK))
+            nc.sync.dma_start(gate_row[0:1, :], gt.rearrange("s o -> o s"))
 
         def load_words():
             nc.sync.dma_start(
@@ -83,22 +85,17 @@ def tile_picked_toklearn_sigmoid_p_kernel(
         load_weight("wa", wa, 0)
         load_weight("wb", wb, 1)
         load_weight("wa", wa, 1)
+        nc.sync.dma_start(place_w[1][:], gt.rearrange("(p t) o -> p (t o)", t=PACK))
 
 
         make_identity(nc, ident[:], nomemset=True)
-        warm = sb([P, 1], F32, "warm")
-        nc.scalar.activation(warm[:], dealt_rows[:, 0, 0:1], ACT.Sigmoid)
-        nc.scalar.copy(
-            dealt_rows[0:2].rearrange("r t (b q) -> r t b q", q=8),
-            rows[:].rearrange("r (b t q) -> r t b q", t=PACK, q=8),
-        )
         gate_bank = psum.tile([P, PACK, CH], F32, name="gate_bank")
         for t in range(PACK):
-            nc.tensor.transpose(gate_bank[:, t, :], dealt_rows[:, t, :], ident[:])
+            nc.tensor.transpose(gate_bank[:, t, :], gate_row[:, t:S:PACK], ident[:])
 
         def gather(table, lst, dst):
             nc.vector.tensor_copy(
-                dst[:].rearrange("p (t b q) -> p b t q", t=PACK, q=8), table[:].indirect(lst[:])
+                dst[:].rearrange("p (t m) -> p m t", t=PACK), table[:].indirect(lst[:])
             )
             return dst
 
@@ -138,24 +135,22 @@ def tile_picked_toklearn_sigmoid_p_kernel(
             return bank
 
         def spread(r):
-            return place_w[:, r, :].unsqueeze(1).to_broadcast([P, CH, PACK])
+            return place_w[r][:].unsqueeze(1).to_broadcast([P, CH, PACK])
 
         val_scales = gather(scale_table, val_list, sb([P, S], U8, "val_scales"))
         map_scales = gather(scale_table, map_list, sb([P, S], U8, "map_scales"))
         wb_g = [cast("wb", 0)]
         wa_g = [cast("wa", 0)]
-        place_w = sb([P, 2, PACK], F32, "place_w", tag="raw_wa0")
         wb_g.append(cast("wb", 1))
         wa_g.append(cast("wa", 1))
         val_words = gather(word_table, val_list, sb([P, S], U32, "val_words"))
         wb_q = [quantize(wb_g[0][:], HALF, "wb0")]
         map_words = gather(word_table, map_list, reused([P, S], U32, "map_words", 8192 + 64 + 1024))
-        nc.vector.tensor_copy(place_w[:], gate_bank[:, :, 0:2].rearrange("p t r -> p r t"))
         wa_q = [quantize(wa_g[0][:], HALF, "wa0")]
         z2_codes = sb([P, N], U32, "values_codes")
         z2_scales = sb([P, N], U8, "values_sc")
 
-        values = [sb([P, HALF, PACK], BF16, "values0"), reused([P, HALF, PACK], BF16, "values1", 3072)]
+        values = [sb([P, HALF, PACK], BF16, "values0", tag="raw_wa0"), reused([P, HALF, PACK], BF16, "values1", 3072)]
 
         def weigh_values(h):
             for i in range(2):
@@ -218,7 +213,7 @@ def tile_picked_toklearn_sigmoid_p_kernel(
                 nc.gpsimd.tensor_tensor(
                     z[c][:, width:, :], maps[c][:, width:, :], spread(1)[:, width:, :], MULT
                 )
-            gate = gate_bank[:, :, 1:2].rearrange("p t o -> p o t").to_broadcast([P, width, PACK])
+            gate = gate_bank[:, :, 0:1].rearrange("p t o -> p o t").to_broadcast([P, width, PACK])
             nc.vector.tensor_tensor(z[c][:, :width, :], maps[c][:, :width, :], gate, MULT)
 
         zq = {}

@@ -49,12 +49,13 @@ def tile_picked_toklearn_sigmoid_p_kernel(
 
         nc.vector.memset(scale_table[:].bitcast(I32), 0)
         ident = sb([P, P], F32, "ident")
-        gate_row = reused([P, S], F32, "gate_row", 8192)
+        gate_row = reused([1, S], F32, "gate_row", 8192)
+        dealt_row = sb([P, PACK, P], F32, "dealt_row")
         place_w = [sb([P, PACK], F32, "place_w%d" % r) for r in range(2)]
         nc.vector.memset(ident[:], 0.0)
-        nc.vector.memset(gate_row[:], 0.0)
+        nc.vector.memset(dealt_row[:], 0.0)
         warm = sb([P, 1], F32, "warm")
-        nc.scalar.activation(warm[:], gate_row[:, 0:1], ACT.Sigmoid)
+        nc.scalar.activation(warm[:], dealt_row[:, 0, 0:1], ACT.Sigmoid)
         raw = {}
 
         def load_weight(name, w, h):
@@ -67,8 +68,8 @@ def tile_picked_toklearn_sigmoid_p_kernel(
             )
 
         def load_gates():
+            nc.sync.dma_start(gate_row[:], gt.rearrange("s o -> o s"))
             nc.sync.dma_start(place_w[0][:], gi.rearrange("(p t) o -> p (t o)", t=PACK))
-            nc.sync.dma_start(gate_row[0:1, :], gt.rearrange("s o -> o s"))
 
         def load_words():
             nc.sync.dma_start(
@@ -89,9 +90,10 @@ def tile_picked_toklearn_sigmoid_p_kernel(
 
 
         make_identity(nc, ident[:], nomemset=True)
+        nc.scalar.copy(dealt_row[0:1].rearrange("r t p -> r p t"), gate_row[:].rearrange("r (p t) -> r p t", t=PACK))
         gate_bank = psum.tile([P, PACK, CH], F32, name="gate_bank")
         for t in range(PACK):
-            nc.tensor.transpose(gate_bank[:, t, :], gate_row[:, t:S:PACK], ident[:])
+            nc.tensor.transpose(gate_bank[:, t, :], dealt_row[:, t, :], ident[:])
 
         def gather(table, lst, dst):
             nc.vector.tensor_copy(

@@ -15,15 +15,17 @@ U8 = mybir.dt.uint8
 FP8X4 = mybir.dt.float8_e4m3fn_x4
 ACT = mybir.ActivationFunctionType
 MULT = mybir.AluOpType.mult
+ADD = mybir.AluOpType.add
 
 P = 128
 PACK = 4
 CH = 128
 HALF = 256
+POOL_CAST = 64
 BANKS = {
     "b": ("b01", "b01", "b2", "b3"),
-    "a": ("a0", "b01", "b01", "b2"),
-    "out": (("r0", "a0"), ("r1",), ("b01", "b3"), ("b01", "b2")),
+    "a": ("a0", "b01", "b01", "r1"),
+    "out": (("r0", "a0"), ("r1", "b01"), ("b01", "b3"), ("b01", "b2")),
 }
 
 
@@ -103,10 +105,15 @@ def tile_picked_toklearn_sigmoid_p_kernel(
 
         def cast(name, h):
             grouped = sb([P, HALF, PACK], BF16, "grouped_%s%d" % (name, h))
+            width = HALF - POOL_CAST if (name, h) == ("wa", 1) else HALF
             nc.scalar.copy(
-                grouped[:].rearrange("p (c i) t -> p c t i", i=4),
-                raw[name, h][:].rearrange("p t (c i) -> p c t i", i=4),
+                grouped[:, :width, :].rearrange("p (c i) t -> p c t i", i=4),
+                raw[name, h][:, :, :width].rearrange("p t (c i) -> p c t i", i=4),
             )
+            if width < HALF:
+                nc.gpsimd.tensor_scalar(
+                    grouped[:, width:, :], raw[name, h][:, :, width:].rearrange("p t c -> p c t"), 1.0, 0.0, MULT, ADD
+                )
             return grouped
 
         def quantize(grouped, width, name):
@@ -150,7 +157,7 @@ def tile_picked_toklearn_sigmoid_p_kernel(
         map_words = gather(word_table, map_list, reused([P, S], U32, "map_words", 8192 + 64 + 1024))
         wa_q = [quantize(wa_g[0][:], HALF, "wa0")]
         z2_codes = sb([P, N], U32, "values_codes")
-        z2_scales = sb([P, N], U8, "values_sc")
+        z2_scales = reused([P, N], U8, "values_sc", 2560)
 
         values = [sb([P, HALF, PACK], BF16, "values0", tag="raw_wa0"), reused([P, HALF, PACK], BF16, "values1", 3072)]
 
@@ -171,8 +178,8 @@ def tile_picked_toklearn_sigmoid_p_kernel(
 
         weigh_values(0)
         wb_q.append(quantize(wb_g[1][:], HALF, "wb1"))
-        quantize_values(0)
         wa_q.append(quantize(wa_g[1][:], HALF, "wa1"))
+        quantize_values(0)
         weigh_values(1)
 
 
@@ -180,7 +187,7 @@ def tile_picked_toklearn_sigmoid_p_kernel(
         for c in range(4):
             bank = first_product(map_words, map_scales, wa_q, c, "a")
             if c < 2:
-                sig = reused([P, CH, PACK], F32, "sig%d" % c, (1024, 5120)[c])
+                sig = reused([P, CH, PACK], F32, "sig%d" % c, (512, 5120)[c])
             else:
                 sig = sb([P, CH, PACK], F32, "sig%d" % c)
             nc.scalar.activation(sig[:], bank[:].rearrange("p t n -> p n t"), ACT.Sigmoid)
@@ -228,7 +235,7 @@ def tile_picked_toklearn_sigmoid_p_kernel(
         def finish(c, which=None):
             codes, scales = zq[c]
             result = results[c]
-            parts = 1 if c == 1 else 2
+            parts = 2
             width = N // parts
             for i in range(parts) if which is None else (which,):
                 cols = slice(i * width, (i + 1) * width)
@@ -242,23 +249,24 @@ def tile_picked_toklearn_sigmoid_p_kernel(
                     start=True,
                     stop=True,
                 )
-                if i == 0 or c == 0:
+                if i == 0 or c < 2:
                     nc.scalar.activation(result[:, cols], acc[:], ACT.Copy, scale=0.0625)
                 else:
                     nc.vector.tensor_scalar_mul(result[:, cols], acc[:], 0.0625)
-                if c % 2 == 0:
+                if c < 3:
                     nc.sync.dma_start(out[c * CH : (c + 1) * CH, cols], result[:, cols])
-            if c % 2 == 1:
+            if c == 3:
                 nc.sync.dma_start(out[c * CH : (c + 1) * CH, :], result[:])
 
         weigh(0)
         weigh(1)
         quantize_map(0)
         finish(0, 0)
+        quantize_map(1)
+        finish(1, 0)
         quantize_values(1)
         finish(0, 1)
-        quantize_map(1)
-        finish(1)
+        finish(1, 1)
         weigh(2)
         weigh(3)
         quantize_map(2)

@@ -63,6 +63,8 @@ def tile_picked_toklearn_sigmoid_p_kernel(
         def load_weight(name, w, h):
             if (name, h) == ("wa", 1):
                 raw[name, h] = reused([P, PACK, HALF], F32, "raw_wa1", 2048)
+            elif (name, h) == ("wb", 0):
+                raw[name, h] = reused([P, PACK, HALF], F32, "raw_wb0", 12288)
             else:
                 raw[name, h] = sb([P, PACK, HALF], F32, "raw_%s%d" % (name, h))
             nc.sync.dma_start(
@@ -73,17 +75,18 @@ def tile_picked_toklearn_sigmoid_p_kernel(
             nc.sync.dma_start(gate_row[:], gt.rearrange("s o -> o s"))
             nc.sync.dma_start(place_w[0][:], gi.rearrange("(p t) o -> p (t o)", t=PACK))
 
-        def load_words():
+        def load_words(lo, hi):
             nc.sync.dma_start(
-                word_table[:].bitcast(I32), x_words[0].rearrange("p c r -> p (c r)").bitcast(I32)
+                word_table[:, lo:hi].bitcast(I32), x_words[0].rearrange("p c r -> p (c r)").bitcast(I32)[:, lo:hi]
             )
 
-        load_weight("wb", wb, 0)
         nc.sync.dma_start(val_list[:], val_l)
+        load_words(0, T // 4)
         nc.sync.dma_start(map_list[:], offs)
         for r in range(4):
             nc.sync.dma_start(scale_table[r:P:32, :].bitcast(I32), x_scales[0, r:16:4, :].bitcast(I32))
-        load_words()
+        load_weight("wb", wb, 0)
+        load_words(T // 4, T)
         load_gates()
         load_weight("wa", wa, 0)
         load_weight("wb", wb, 1)
@@ -117,10 +120,7 @@ def tile_picked_toklearn_sigmoid_p_kernel(
             return grouped
 
         def quantize(grouped, width, name):
-            if name == "wb0":
-                codes = reused([P, width], U32, "wb0_codes", 8192 - 960)
-            else:
-                codes = sb([P, width], U32, name + "_codes")
+            codes = sb([P, width], U32, name + "_codes")
             scales = sb([P, width], U8, name + "_sc")
             nc.vector.quantize_mx(
                 out=codes[:].bitcast(FP8X4), scales=scales[:], in_=grouped.rearrange("p c t -> p (c t)")
@@ -152,12 +152,12 @@ def tile_picked_toklearn_sigmoid_p_kernel(
         wa_g = [cast("wa", 0)]
         wb_g.append(cast("wb", 1))
         wa_g.append(cast("wa", 1))
-        val_words = gather(word_table, val_list, sb([P, S], U32, "val_words"))
         wb_q = [quantize(wb_g[0][:], HALF, "wb0")]
-        map_words = gather(word_table, map_list, reused([P, S], U32, "map_words", 8192 + 64 + 1024))
+        val_words = gather(word_table, val_list, reused([P, S], U32, "val_words", 12288))
+        map_words = gather(word_table, map_list, reused([P, S], U32, "map_words", 12288 + 2048))
         wa_q = [quantize(wa_g[0][:], HALF, "wa0")]
         z2_codes = sb([P, N], U32, "values_codes")
-        z2_scales = reused([P, N], U8, "values_sc", 2560)
+        z2_scales = sb([P, N], U8, "values_sc")
 
         values = [sb([P, HALF, PACK], BF16, "values0", tag="raw_wa0"), reused([P, HALF, PACK], BF16, "values1", 3072)]
 
@@ -178,8 +178,8 @@ def tile_picked_toklearn_sigmoid_p_kernel(
 
         weigh_values(0)
         wb_q.append(quantize(wb_g[1][:], HALF, "wb1"))
-        wa_q.append(quantize(wa_g[1][:], HALF, "wa1"))
         quantize_values(0)
+        wa_q.append(quantize(wa_g[1][:], HALF, "wa1"))
         weigh_values(1)
 
 

@@ -186,8 +186,10 @@ def tile_picked_toklearn_sigmoid_p_kernel(
         maps = []
         for c in range(4):
             bank = first_product(map_words, map_scales, wa_q, c, "a")
-            if c < 2:
-                sig = reused([P, CH, PACK], F32, "sig%d" % c, (512, 5120)[c])
+            if c == 0:
+                sig = sb([P, CH, PACK], F32, "sig0", tag="grouped_wb1")
+            elif c == 1:
+                sig = reused([P, CH, PACK], F32, "sig1", 5120)
             else:
                 sig = sb([P, CH, PACK], F32, "sig%d" % c)
             nc.scalar.activation(sig[:], bank[:].rearrange("p t n -> p n t"), ACT.Sigmoid)

@@ -21,7 +21,6 @@ P = 128
 PACK = 4
 CH = 128
 HALF = 256
-POOL_CAST = 64
 BANKS = {
     "b": ("b01", "b01", "b2", "b3"),
     "a": ("a0", "b01", "b01", "r1"),
@@ -62,8 +61,15 @@ def tile_picked_toklearn_sigmoid_p_kernel(
 
         def load_weight(name, w, h):
             if (name, h) == ("wa", 1):
-                raw[name, h] = reused([P, PACK, HALF], F32, "raw_wa1", 2048)
-            elif (name, h) == ("wb", 0):
+                for q in range(2):
+                    if q == 0:
+                        raw[name, h, q] = sb([P, PACK, CH], F32, "raw_wa1a")
+                    else:
+                        raw[name, h, q] = reused([P, PACK, CH], F32, "raw_wa1b", 4096)
+                    lo = HALF + q * CH
+                    nc.sync.dma_start(raw[name, h, q][:], w[:, lo : lo + CH].rearrange("(p j) c -> p j c", j=PACK))
+                return
+            if (name, h) == ("wb", 0):
                 raw[name, h] = reused([P, PACK, HALF], F32, "raw_wb0", 12288)
             else:
                 raw[name, h] = sb([P, PACK, HALF], F32, "raw_%s%d" % (name, h))
@@ -108,15 +114,19 @@ def tile_picked_toklearn_sigmoid_p_kernel(
 
         def cast(name, h):
             grouped = sb([P, HALF, PACK], BF16, "grouped_%s%d" % (name, h))
-            width = HALF - POOL_CAST if (name, h) == ("wa", 1) else HALF
-            nc.scalar.copy(
-                grouped[:, :width, :].rearrange("p (c i) t -> p c t i", i=4),
-                raw[name, h][:, :, :width].rearrange("p t (c i) -> p c t i", i=4),
-            )
-            if width < HALF:
+            if (name, h) == ("wa", 1):
                 nc.gpsimd.tensor_scalar(
-                    grouped[:, width:, :], raw[name, h][:, :, width:].rearrange("p t c -> p c t"), 1.0, 0.0, MULT, ADD
+                    grouped[:, :CH, :], raw[name, h, 0][:].rearrange("p t c -> p c t"), 1.0, 0.0, MULT, ADD
                 )
+                nc.scalar.copy(
+                    grouped[:, CH:, :].rearrange("p (c i) t -> p c t i", i=4),
+                    raw[name, h, 1][:].rearrange("p t (c i) -> p c t i", i=4),
+                )
+                return grouped
+            nc.scalar.copy(
+                grouped[:].rearrange("p (c i) t -> p c t i", i=4),
+                raw[name, h][:].rearrange("p t (c i) -> p c t i", i=4),
+            )
             return grouped
 
         def quantize(grouped, width, name):

@@ -123,18 +123,26 @@ def tile_picked_toklearn_sigmoid_p_kernel(
                     raw[name, h, 1][:].rearrange("p t (c i) -> p c t i", i=4),
                 )
                 return grouped
-            nc.scalar.copy(
-                grouped[:].rearrange("p (c i) t -> p c t i", i=4),
-                raw[name, h][:].rearrange("p t (c i) -> p c t i", i=4),
-            )
+            pieces = 2 if (name, h) == ("wa", 0) else 1
+            for q in range(pieces):
+                cols = slice(q * HALF // pieces, (q + 1) * HALF // pieces)
+                nc.scalar.copy(
+                    grouped[:, cols, :].rearrange("p (c i) t -> p c t i", i=4),
+                    raw[name, h][:, :, cols].rearrange("p t (c i) -> p c t i", i=4),
+                )
             return grouped
 
         def quantize(grouped, width, name):
             codes = sb([P, width], U32, name + "_codes")
             scales = sb([P, width], U8, name + "_sc")
-            nc.vector.quantize_mx(
-                out=codes[:].bitcast(FP8X4), scales=scales[:], in_=grouped.rearrange("p c t -> p (c t)")
-            )
+            pieces = 2 if name == "wa0" else 1
+            for q in range(pieces):
+                cols = slice(q * width // pieces, (q + 1) * width // pieces)
+                nc.vector.quantize_mx(
+                    out=codes[:, cols].bitcast(FP8X4),
+                    scales=scales[:, cols],
+                    in_=grouped[:, cols, :].rearrange("p c t -> p (c t)"),
+                )
             return codes, scales
 
         def first_product(words, scales, wq, c, tag):

@@ -21,6 +21,8 @@ P = 128
 PACK = 4
 CH = 128
 HALF = 256
+POOL_CAST = 96
+POOL_FIRST = 112
 BANKS = {
     "b": ("b01", "b01", "b2", "b3"),
     "a": ("a0", "b01", "b01", "r1"),
@@ -116,7 +118,16 @@ def tile_picked_toklearn_sigmoid_p_kernel(
             grouped = sb([P, HALF, PACK], BF16, "grouped_%s%d" % (name, h))
             if (name, h) == ("wa", 1):
                 nc.gpsimd.tensor_scalar(
-                    grouped[:, :CH, :], raw[name, h, 0][:].rearrange("p t c -> p c t"), 1.0, 0.0, MULT, ADD
+                    grouped[:, :POOL_CAST, :],
+                    raw[name, h, 0][:, :, :POOL_CAST].rearrange("p t c -> p c t"),
+                    1.0,
+                    0.0,
+                    MULT,
+                    ADD,
+                )
+                nc.scalar.copy(
+                    grouped[:, POOL_CAST:CH, :].rearrange("p (c i) t -> p c t i", i=4),
+                    raw[name, h, 0][:, :, POOL_CAST:].rearrange("p t (c i) -> p c t i", i=4),
                 )
                 nc.scalar.copy(
                     grouped[:, CH:, :].rearrange("p (c i) t -> p c t i", i=4),
@@ -135,7 +146,7 @@ def tile_picked_toklearn_sigmoid_p_kernel(
         def quantize(grouped, width, name):
             codes = sb([P, width], U32, name + "_codes")
             scales = sb([P, width], U8, name + "_sc")
-            pieces = 2 if name == "wa0" else 1
+            pieces = 2 if name[0:2] == "wa" else 1
             for q in range(pieces):
                 cols = slice(q * width // pieces, (q + 1) * width // pieces)
                 nc.vector.quantize_mx(
@@ -230,7 +241,11 @@ def tile_picked_toklearn_sigmoid_p_kernel(
         def weigh(c):
             if c == 0:
                 z[c] = sb([P, CH, PACK], BF16, "z0", tag="grouped_wa1")
-                nc.gpsimd.tensor_tensor(z[c][:], maps[c][:], spread(1), MULT)
+                nc.gpsimd.tensor_tensor(
+                    z[c][:, :POOL_FIRST, :], maps[c][:, :POOL_FIRST, :], spread(1)[:, :POOL_FIRST, :], MULT
+                )
+                gate = gate_bank[:, :, 0:1].rearrange("p t o -> p o t").to_broadcast([P, CH - POOL_FIRST, PACK])
+                nc.vector.tensor_tensor(z[c][:, POOL_FIRST:, :], maps[c][:, POOL_FIRST:, :], gate, MULT)
                 return
             if c == 3:
                 z[c] = reused([P, CH, PACK], BF16, "z3", 3072)

@@ -224,18 +224,6 @@ def tile_picked_toklearn_sigmoid_p_kernel(
             nc.scalar.activation(sig[:], bank[:].rearrange("p t n -> p n t"), ACT.Sigmoid)
             maps.append(sig)
 
-        idle_bank = psum.tile([P, 2, HALF], F32, name="idle_bank", tag="b3")
-        for i in range(2):
-            nc.tensor.matmul_mx(
-                out=idle_bank[:, i, :],
-                lhsT=wa_q[1][0][:, i * CH : (i + 1) * CH].bitcast(FP8X4),
-                lhsT_scale=wa_q[1][1][:, i * CH : (i + 1) * CH],
-                rhs=wb_q[i][0][:].bitcast(FP8X4),
-                rhs_scale=wb_q[i][1][:],
-                start=True,
-                stop=True,
-            )
-
         z = {}
 
         def weigh(c):

from contextlib import ExitStack

import concourse.mybir as mybir
from concourse.masks import make_identity

K, T, S, N, H = 512, 2048, 512, 512, 512
FLOPS = 2 * S * K * H + 2 * S * K * N + 2 * H * S * N

F32 = mybir.dt.float32
BF16 = mybir.dt.bfloat16
I32 = mybir.dt.int32
U32 = mybir.dt.uint32
U16 = mybir.dt.uint16
U8 = mybir.dt.uint8
FP8X4 = mybir.dt.float8_e4m3fn_x4
ACT = mybir.ActivationFunctionType
MULT = mybir.AluOpType.mult
ADD = mybir.AluOpType.add

P = 128
PACK = 4
CH = 128
HALF = 256
POOL_CAST = 96
POOL_FIRST = 112
BANKS = {
    "b": ("b01", "b01", "b2", "b3"),
    "a": ("a0", "b01", "b01", "r1"),
    "out": (("r0", "a0"), ("r1", "b01"), ("b01", "b3"), ("b01", "b2")),
}


def tile_picked_toklearn_sigmoid_p_kernel(
    tc, x_words, x_scales, wa, wb, gt, gi, offs, val_l, out
):
    nc = tc.nc
    with ExitStack() as ctx:
        keep = ctx.enter_context(tc.tile_pool(name="keep", bufs=1))
        shared = ctx.enter_context(tc.tile_pool(name="shared", bufs=1))
        psum = ctx.enter_context(tc.psum_pool(name="psum", bufs=1))

        def sb(shape, dtype, name, tag=None):
            return keep.tile(shape, dtype, name=name, tag=tag or name, align_bytes=64)

        def reused(shape, dtype, name, offset):
            return shared.tile(shape, dtype, name=name, offset=offset, align_bytes=64)

        val_list = sb([P, S // 16], U16, "val_list")
        map_list = sb([P, S // 16], U16, "map_list")
        scale_table = sb([P, T], U8, "scale_table")
        word_table = sb([P, T], U32, "word_table")

        nc.vector.memset(scale_table[:].bitcast(I32), 0)
        ident = sb([P, P], F32, "ident")
        gate_row = reused([1, S], F32, "gate_row", 8192)
        dealt_row = sb([P, PACK, P], F32, "dealt_row")
        place_w = [sb([P, PACK], F32, "place_w%d" % r) for r in range(2)]
        nc.vector.memset(ident[:], 0.0)
        nc.vector.memset(dealt_row[:], 0.0)
        warm = sb([P, 1], F32, "warm")
        nc.scalar.activation(warm[:], dealt_row[:, 0, 0:1], ACT.Sigmoid)
        raw = {}

        def load_weight(name, w, h):
            if (name, h) == ("wa", 1):
                for q in range(2):
                    if q == 0:
                        raw[name, h, q] = sb([P, PACK, CH], F32, "raw_wa1a")
                    else:
                        raw[name, h, q] = reused([P, PACK, CH], F32, "raw_wa1b", 4096)
                    lo = HALF + q * CH
                    nc.sync.dma_start(raw[name, h, q][:], w[:, lo : lo + CH].rearrange("(p j) c -> p j c", j=PACK))
                return
            if (name, h) == ("wb", 0):
                raw[name, h] = reused([P, PACK, HALF], F32, "raw_wb0", 12288)
            else:
                raw[name, h] = sb([P, PACK, HALF], F32, "raw_%s%d" % (name, h))
            nc.sync.dma_start(
                raw[name, h][:], w[:, h * HALF : (h + 1) * HALF].rearrange("(p j) c -> p j c", j=PACK)
            )

        def load_gates():
            nc.sync.dma_start(gate_row[:], gt.rearrange("s o -> o s"))
            nc.sync.dma_start(place_w[0][:], gi.rearrange("(p t) o -> p (t o)", t=PACK))

        def load_words(lo, hi):
            nc.sync.dma_start(
                word_table[:, lo:hi].bitcast(I32), x_words[0].rearrange("p c r -> p (c r)").bitcast(I32)[:, lo:hi]
            )

        nc.sync.dma_start(val_list[:], val_l)
        load_words(0, T // 4)
        nc.sync.dma_start(map_list[:], offs)
        for r in range(4):
            nc.sync.dma_start(scale_table[r:P:32, :].bitcast(I32), x_scales[0, r:16:4, :].bitcast(I32))
        load_weight("wb", wb, 0)
        load_words(T // 4, T)
        load_gates()
        load_weight("wa", wa, 0)
        load_weight("wb", wb, 1)
        load_weight("wa", wa, 1)
        nc.sync.dma_start(place_w[1][:], gt.rearrange("(p t) o -> p (t o)", t=PACK))


        make_identity(nc, ident[:], nomemset=True)
        nc.scalar.copy(dealt_row[0:1].rearrange("r t p -> r p t"), gate_row[:].rearrange("r (p t) -> r p t", t=PACK))
        gate_bank = psum.tile([P, PACK, CH], F32, name="gate_bank")
        for t in range(PACK):
            nc.tensor.transpose(gate_bank[:, t, :], dealt_row[:, t, :], ident[:])

        def gather(table, lst, dst):
            nc.vector.tensor_copy(
                dst[:].rearrange("p (t m) -> p m t", t=PACK), table[:].indirect(lst[:])
            )
            return dst

        def cast(name, h):
            grouped = sb([P, HALF, PACK], BF16, "grouped_%s%d" % (name, h))
            if (name, h) == ("wa", 1):
                nc.gpsimd.tensor_scalar(
                    grouped[:, :POOL_CAST, :],
                    raw[name, h, 0][:, :, :POOL_CAST].rearrange("p t c -> p c t"),
                    1.0,
                    0.0,
                    MULT,
                    ADD,
                )
                nc.scalar.copy(
                    grouped[:, POOL_CAST:CH, :].rearrange("p (c i) t -> p c t i", i=4),
                    raw[name, h, 0][:, :, POOL_CAST:].rearrange("p t (c i) -> p c t i", i=4),
                )
                nc.scalar.copy(
                    grouped[:, CH:, :].rearrange("p (c i) t -> p c t i", i=4),
                    raw[name, h, 1][:].rearrange("p t (c i) -> p c t i", i=4),
                )
                return grouped
            pieces = 2 if (name, h) == ("wa", 0) else 1
            for q in range(pieces):
                cols = slice(q * HALF // pieces, (q + 1) * HALF // pieces)
                nc.scalar.copy(
                    grouped[:, cols, :].rearrange("p (c i) t -> p c t i", i=4),
                    raw[name, h][:, :, cols].rearrange("p t (c i) -> p c t i", i=4),
                )
            return grouped

        def quantize(grouped, width, name):
            codes = sb([P, width], U32, name + "_codes")
            scales = sb([P, width], U8, name + "_sc")
            pieces = 2 if name[0:2] == "wa" else 1
            for q in range(pieces):
                cols = slice(q * width // pieces, (q + 1) * width // pieces)
                nc.vector.quantize_mx(
                    out=codes[:, cols].bitcast(FP8X4),
                    scales=scales[:, cols],
                    in_=grouped[:, cols, :].rearrange("p c t -> p (c t)"),
                )
            return codes, scales

        def first_product(words, scales, wq, c, tag):
            codes, wscales = wq[c // 2]
            cols = slice((c % 2) * CH, (c % 2 + 1) * CH)
            bank = psum.tile([P, PACK, CH], F32, name="bank_%s%d" % (tag, c), tag=BANKS[tag][c], bufs=2 if BANKS[tag][c] == "b01" else 1)
            for t in range(PACK):
                nc.tensor.matmul_mx(
                    out=bank[:, t, :],
                    lhsT=words[:, t * P : (t + 1) * P].bitcast(FP8X4),
                    lhsT_scale=scales[:, t * P : (t + 1) * P],
                    rhs=codes[:, cols].bitcast(FP8X4),
                    rhs_scale=wscales[:, cols],
                    start=True,
                    stop=True,
                )
            return bank

        def spread(r):
            return place_w[r][:].unsqueeze(1).to_broadcast([P, CH, PACK])

        val_scales = gather(scale_table, val_list, sb([P, S], U8, "val_scales"))
        map_scales = gather(scale_table, map_list, sb([P, S], U8, "map_scales"))
        wb_g = [cast("wb", 0)]
        wa_g = [cast("wa", 0)]
        wb_g.append(cast("wb", 1))
        wa_g.append(cast("wa", 1))
        wb_q = [quantize(wb_g[0][:], HALF, "wb0")]
        val_words = gather(word_table, val_list, reused([P, S], U32, "val_words", 12288))
        map_words = gather(word_table, map_list, reused([P, S], U32, "map_words", 12288 + 2048))
        wa_q = [quantize(wa_g[0][:], HALF, "wa0")]
        z2_codes = sb([P, N], U32, "values_codes")
        z2_scales = sb([P, N], U8, "values_sc")

        values = [sb([P, HALF, PACK], BF16, "values0", tag="raw_wa0"), reused([P, HALF, PACK], BF16, "values1", 3072)]

        def weigh_values(h):
            for i in range(2):
                bank = first_product(val_words, val_scales, wb_q, 2 * h + i, "b")
                nc.vector.tensor_tensor(
                    values[h][:, i * CH : (i + 1) * CH, :], bank[:].rearrange("p t n -> p n t"), spread(0), MULT
                )

        def quantize_values(h):
            cols = slice(h * HALF, (h + 1) * HALF)
            nc.vector.quantize_mx(
                out=z2_codes[:, cols].bitcast(FP8X4),
                scales=z2_scales[:, cols],
                in_=values[h][:].rearrange("p c t -> p (c t)"),
            )

        weigh_values(0)
        wb_q.append(quantize(wb_g[1][:], HALF, "wb1"))
        quantize_values(0)
        wa_q.append(quantize(wa_g[1][:], HALF, "wa1"))
        weigh_values(1)


        maps = []
        for c in range(4):
            bank = first_product(map_words, map_scales, wa_q, c, "a")
            if c == 0:
                sig = sb([P, CH, PACK], F32, "sig0", tag="grouped_wb1")
            elif c == 1:
                sig = reused([P, CH, PACK], F32, "sig1", 5120)
            else:
                sig = sb([P, CH, PACK], F32, "sig%d" % c)
            nc.scalar.activation(sig[:], bank[:].rearrange("p t n -> p n t"), ACT.Sigmoid)
            maps.append(sig)

        z = {}

        def weigh(c):
            if c == 0:
                z[c] = sb([P, CH, PACK], BF16, "z0", tag="grouped_wa1")
                nc.gpsimd.tensor_tensor(
                    z[c][:, :POOL_FIRST, :], maps[c][:, :POOL_FIRST, :], spread(1)[:, :POOL_FIRST, :], MULT
                )
                gate = gate_bank[:, :, 0:1].rearrange("p t o -> p o t").to_broadcast([P, CH - POOL_FIRST, PACK])
                nc.vector.tensor_tensor(z[c][:, POOL_FIRST:, :], maps[c][:, POOL_FIRST:, :], gate, MULT)
                return
            if c == 3:
                z[c] = reused([P, CH, PACK], BF16, "z3", 3072)
            else:
                z[c] = sb([P, CH, PACK], BF16, "z%d" % c)
            width = CH
            if c == 3:
                width = CH // 2
                nc.gpsimd.tensor_tensor(
                    z[c][:, width:, :], maps[c][:, width:, :], spread(1)[:, width:, :], MULT
                )
            gate = gate_bank[:, :, 0:1].rearrange("p t o -> p o t").to_broadcast([P, width, PACK])
            nc.vector.tensor_tensor(z[c][:, :width, :], maps[c][:, :width, :], gate, MULT)

        zq = {}
        results = {}

        def quantize_map(c):
            zq[c] = quantize(z[c][:], CH, "z%d" % c)
            results[c] = sb([P, N], F32, "result%d" % c)

        def finish(c, which=None):
            codes, scales = zq[c]
            result = results[c]
            parts = 2
            width = N // parts
            for i in range(parts) if which is None else (which,):
                cols = slice(i * width, (i + 1) * width)
                acc = psum.tile([P, width], F32, name="acc%d_%d" % (c, i), tag=BANKS["out"][c][i], bufs=2 if BANKS["out"][c][i] == "b01" else 1)
                nc.tensor.matmul_mx(
                    out=acc[:],
                    lhsT=codes[:].bitcast(FP8X4),
                    lhsT_scale=scales[:],
                    rhs=z2_codes[:, cols].bitcast(FP8X4),
                    rhs_scale=z2_scales[:, cols],
                    start=True,
                    stop=True,
                )
                if i == 0 or c < 2:
                    nc.scalar.activation(result[:, cols], acc[:], ACT.Copy, scale=0.0625)
                else:
                    nc.vector.tensor_scalar_mul(result[:, cols], acc[:], 0.0625)
                if c < 3:
                    nc.sync.dma_start(out[c * CH : (c + 1) * CH, cols], result[:, cols])
            if c == 3:
                nc.sync.dma_start(out[c * CH : (c + 1) * CH, :], result[:])

        weigh(0)
        weigh(1)
        quantize_map(0)
        finish(0, 0)
        quantize_map(1)
        finish(1, 0)
        quantize_values(1)
        finish(0, 1)
        finish(1, 1)
        weigh(2)
        weigh(3)
        quantize_map(2)
        quantize_map(3)
        finish(2)
        finish(3)
